import numpy as np, ml_dtypes
CORES = [4,12,20,28,44,60,76,84,92,108,116,124]
N = 12
DEG, TK = 5, 128
MASK = [[10,11,0,1,2],[11,0,1,2,3],[0,1,2,3,4],[1,2,3,4,5],[2,3,4,5,6],[3,4,5,6,7],[4,5,6,7,8],[5,6,7,8,9],[6,7,8,9,10],[7,8,9,10,11],[8,9,10,11,0],[9,10,11,0,1]]
def setup_inputs(rng):
    return {"x": rng.standard_normal((N, 128, TK), dtype=np.float32).astype(ml_dtypes.bfloat16), "w": rng.standard_normal((N, 128, DEG * 128), dtype=np.float32).astype(ml_dtypes.bfloat16)}
def setup_inputs_big(rng):
    d = setup_inputs(rng)
    for k in ("x", "w"): d[k] = (d[k].astype(np.float32) * 1024.0).astype(d[k].dtype)
    return d
def setup_inputs_small(rng):
    d = setup_inputs(rng)
    for k in ("x", "w"): d[k] = (d[k].astype(np.float32) * (1 / 1024.0)).astype(d[k].dtype)
    return d
def setup_inputs_apart(rng):
    d = setup_inputs(rng)
    f = (10.0 ** rng.permutation(np.linspace(-1.5, 1.5, N))).astype(np.float32).reshape(N, 1, 1)
    for k in ("x", "w"): d[k] = (d[k].astype(np.float32) * f).astype(d[k].dtype)
    return d
def reference(x, w):
    X, W = x.astype(np.float64), w.astype(np.float64)
    y = np.zeros((N, 128, TK))
    for r in range(N):
        for i, j in enumerate(MASK[r]):
            y[r] += W[r][:, 128 * i:128 * i + 128].T @ X[j]
    return {"y": y.astype(ml_dtypes.bfloat16 if x.dtype != np.float64 else np.float64)}

from concourse.bass import DstId, RemoteDMATransfer

N, DEG, TK = 12, 5, 128
HOP1_ENGINES = 8

SCRATCH = {
    "xd": ("dram", [128, TK], "bfloat16"),
    "hl": ("dram", [128, TK], "bfloat16"),
    "xin": ("sbuf", [128, DEG * TK], "bfloat16"),
    "wsb": ("sbuf", [128, DEG * TK], "bfloat16"),
    "ysb": ("sbuf", [128, TK], "bfloat16"),
    "ps": ("psum", [128, TK], "float32"),
}
SEMAPHORES = ["ld_d", "ld_s", "ld_w", "h", "sent", "mm", "cp", "st"] + ["s%d" % j for j in range(N)]

_CACHE = {}


def _bits(mask):
    n = 0
    while mask:
        n += mask & 1
        mask >>= 1
    return n


def _low(mask, k):
    out, b = 0, 1
    while k and b <= mask:
        if mask & b:
            out |= b
            k -= 1
        b <<= 1
    return out


def _product(lists):
    out = [[]]
    for one in lists:
        out = [p + [o] for p in out for o in one]
    return out


def _links(topo, src_chip, d, dst_chip):
    out, here = [], src_chip
    if here != dst_chip and not topo.same_plane(here, dst_chip):
        out.append(("mate", here, d))
        here = [c for c in range(topo.CHIPS) if topo.mates(here, c)][0]
    if here != dst_chip:
        out.append(("sw_out", here, d))
        out.append(("sw_in", dst_chip, d))
    return out


def _plan(cores, table, topo):
    n = len(cores)
    dests = [[] for _ in range(n)]
    for r in range(n):
        for i, j in enumerate(table[r]):
            if j != r:
                dests[j].append((r, i))
    all_cores = range(topo.CHIPS * topo.CORES_PER_CHIP)
    dies = sorted({topo.die(c) for c in all_cores})

    def options(j):
        me = cores[j]
        pool = [c for c in all_cores if topo.chip(c) == topo.chip(me) and c not in cores]
        direct = [topo.may_write(me, cores[r]) for r, _ in dests[j]]
        per = [[("relay", d) for d in dies] + ([("self", topo.die(me))] if ok else []) for ok in direct]
        res = []
        for combo in _product(per):
            if sum(1 for o in combo if o[0] == "self") != min(1, sum(direct)):
                continue
            free, who, ok = list(pool), {}, True
            order = sorted(range(len(combo)),
                           key=lambda t: sum(1 for c in pool if topo.may_write(c, cores[dests[j][t][0]])))
            for t in order:
                if combo[t][0] == "self":
                    who[t] = me
                    continue
                cand = [c for c in free if topo.die(c) == combo[t][1] and topo.may_write(c, cores[dests[j][t][0]])]
                if not cand:
                    ok = False
                    break
                cand.sort(key=lambda c: (sum(1 for q in cores if topo.may_write(c, q)), c))
                who[t] = cand[0]
                free.remove(cand[0])
            if ok:
                res.append((combo, [who[t] for t in range(len(combo))]))
        return res

    opts = [options(j) for j in range(n)]
    choice = [0] * n

    def cost():
        rel, tot = {}, {}
        for j in range(n):
            combo = opts[j][choice[j]][0]
            for (r, _), o in zip(dests[j], combo):
                for l in _links(topo, topo.chip(cores[j]), o[1], topo.chip(cores[r])):
                    tot[l] = tot.get(l, 0) + 1
                    if o[0] == "relay":
                        rel[l] = rel.get(l, 0) + 1
        return (max(rel.values()), sum(v * v for v in rel.values()),
                max(tot.values()), sum(v * v for v in tot.values()))

    best, changed = cost(), True
    while changed:
        changed = False
        for j in range(n):
            for k in range(len(opts[j])):
                old = choice[j]
                choice[j] = k
                c = cost()
                if c < best:
                    best, changed = c, True
                else:
                    choice[j] = old

    relay = {}
    fan = [[] for _ in range(n)]
    own = [[] for _ in range(n)]
    when = [[] for _ in range(n)]
    for j in range(n):
        combo, who = opts[j][choice[j]]
        todo = []
        for (r, i), o, c in zip(dests[j], combo, who):
            hops = len(_links(topo, topo.chip(cores[j]), o[1], topo.chip(cores[r])))
            if o[0] == "self":
                own[j].append((r, i))
                when[r].append(((0, 0, hops), i, j))
            else:
                todo.append((-hops, c, r, i))
        for pos, (nh, c, r, i) in enumerate(sorted(todo)):
            fan[j].append(c)
            relay[c] = (j, r, i)
            when[r].append(((1, pos, -nh), i, j))
    return {"relay": relay, "fan": fan, "own": own, "when": [sorted(w) for w in when]}


def rank_program(g, core, T, topo):
    if "plan" not in _CACHE:
        _CACHE["plan"] = _plan(list(T.cores), T.tables["MASK"], topo)
    plan = _CACHE["plan"]
    sem = T.sem

    def slot(buf, i):
        return buf[:, i * TK:(i + 1) * TK]

    def fan_mask(j):
        me, m = T.cores[j], -1
        for c in plan["fan"][j] + [T.cores[r] for r, _ in plan["own"][j]]:
            m &= topo.mask(me, c)
        return _low(m, HOP1_ENGINES)

    if core in plan["relay"]:
        j, r, i = plan["relay"][core]
        dst = T.cores[r]
        rid, pid, _ = topo.addr(dst)
        m = topo.mask(core, dst)
        g.wait_ge(sem.h, _bits(fan_mask(j)))
        g.remote_dma(out_ap=slot(T.xin, i), in_ap=T.hl[:, :], remote_sem=sem["s%d" % j], local_sem=sem.sent,
                     pid=pid, routing_id=rid, dma_engine_mask=m)
        g.wait_ge(sem.sent, _bits(m))
        return

    rank = T.rank_of(core)
    if rank is None:
        return
    row = T.tables["MASK"][rank]

    g.sync.dma_start(T.xd[:, :], T.x[:, :]).then_inc(sem.ld_d, 16)
    steps = []
    if rank in row:
        g.sync.dma_start(slot(T.xin, row.index(rank)), T.x[:, :]).then_inc(sem.ld_s, 16)
        steps.append((sem.ld_s, 16, row.index(rank)))
    g.sync.dma_start(T.wsb[:, :], T.w[:, :]).then_inc(sem.ld_w, 16)

    g.wait_ge(sem.ld_d, 16)
    sent = 0
    if plan["fan"][rank]:
        m = fan_mask(rank)
        ids = []
        for c in plan["fan"][rank]:
            rid, pid, _ = topo.addr(c)
            ids.append(DstId(rid=rid, pnc=pid))
        g.remote_dma_fused([RemoteDMATransfer(dst_ids=ids, dma_engine_mask=m, remote_sem=sem.h,
                                              srcs=[T.xd[:, :]], dsts=[T.hl[:, :] for _ in ids], alu_op=0)],
                           local_sem=sem.sent)
        sent += _bits(m)
    for r, i in plan["own"][rank]:
        dst = T.cores[r]
        rid, pid, _ = topo.addr(dst)
        m = topo.mask(core, dst)
        g.remote_dma(out_ap=slot(T.xin, i), in_ap=T.xd[:, :], remote_sem=sem["s%d" % rank], local_sem=sem.sent,
                     pid=pid, routing_id=rid, dma_engine_mask=m)
        sent += _bits(m)
    if sent:
        g.wait_ge(sem.sent, sent)

    for _, i, j in plan["when"][rank]:
        issuer = [c for c in plan["relay"] if plan["relay"][c] == (j, rank, i)] + [T.cores[j]]
        steps.append((sem["s%d" % j], _bits(topo.mask(issuer[0], core)), i))
    g.tensor.wait_ge(sem.ld_w, 16)
    last = None
    for k, (s, cnt, i) in enumerate(steps):
        g.tensor.wait_ge(s, cnt)
        last = g.tensor.matmul(T.ps[:, :], slot(T.wsb, i), slot(T.xin, i), k == 0, k == len(steps) - 1)
    last.then_inc(sem.mm, 1)

    g.vector.wait_ge(sem.mm, 1)
    g.vector.tensor_copy(T.ysb[:, :], T.ps[:, :]).then_inc(sem.cp, 1)
    g.scalar.wait_ge(sem.cp, 1)
    g.scalar.dma_start(T.y[:, :], T.ysb[:, :]).then_inc(sem.st, 16)
    g.scalar.wait_ge(sem.st, 16)
